import numpy as np
import ml_dtypes


def mxq(x, axis, fmt="e4m3"):
    dtype, down = {"e4m3": (ml_dtypes.float8_e4m3fn, 7), "e5m2": (ml_dtypes.float8_e5m2, 14)}[fmt]
    v = np.moveaxis(np.asarray(x, np.float32).astype(ml_dtypes.bfloat16).astype(np.float64), axis, -1)
    blocks = v.reshape(v.shape[:-1] + (-1, 32))
    amax = np.abs(blocks).max(-1, keepdims=True)
    byte = np.maximum(np.where(amax > 0, np.frexp(amax)[1] - 1 + 127, 0) - down, 1)
    scale = np.exp2(byte - 127.0)
    codes = (blocks / scale).astype(np.float32).astype(dtype).astype(np.float64)
    return np.moveaxis((codes * scale).reshape(v.shape), -1, axis)


WIDE = False


def mx_kscale(k):
    if not WIDE:
        return np.ones(k)
    levels = np.array([10, -10, 5, -5, 0])
    if k % 512:
        return np.exp2(np.random.permutation(np.resize(levels, k // 32))).repeat(32)
    a = np.empty((k // 512, 16))
    for p in range(k // 512):
        a[p, :8] = np.random.permutation(np.resize(levels, 8))
        for g in range(8):
            far = levels[np.abs(levels - a[p, g]) >= 10]
            a[p, g + 8] = far[np.random.randint(len(far))]
    return np.exp2(a.ravel()).repeat(32)


def f64(x):
    return np.asarray(x).astype(np.float64)


def striped(idx):
    return np.tile(idx.reshape(-1, 16).T, (8, 1)).astype(np.uint16)


def unstriped(offs):
    return offs[:16].T.reshape(-1).astype(np.int64)


E2M1 = np.array([0.0, 0.5, 1.0, 1.5, 2.0, 3.0, 4.0, 6.0, -0.0, -0.5, -1.0, -1.5, -2.0, -3.0, -4.0, -6.0])


def pack_weight(w, fmt):
    k, n = w.shape
    w = f64(np.asarray(w, np.float32).astype(ml_dtypes.bfloat16)).reshape(k // 32, 32, n)
    amax = np.abs(w).max(1)
    if fmt == "e4m3":
        byte = np.frexp(amax)[1] - 1 + 127 - 7
    else:
        mant, ex = np.frexp(amax / 6.0)
        byte = np.where(mant > 0.5, ex, ex - 1) + 127
    byte = np.clip(np.where(amax > 0, byte, 1), 1, 254)
    scaled = (w * np.exp2(127.0 - byte)[:, None, :]).reshape(k, n).astype(np.float32)
    by_word = np.ascontiguousarray(scaled.reshape(k // 512, 128, 4, n).transpose(0, 1, 3, 2))
    if fmt == "e4m3":
        words = by_word.astype(ml_dtypes.float8_e4m3fn).view(np.uint8)
    else:
        c = by_word.astype(ml_dtypes.float4_e2m1fn).view(np.uint8) & 0xF
        words = (c[..., 0::2] | (c[..., 1::2] << 4)).reshape(k // 512, 128, 2 * n)
    return np.ascontiguousarray(words), np.ascontiguousarray(byte.astype(np.uint8).reshape(k // 512, 16, n))


def unpack_weight(words, scales, fmt):
    g, _, n = scales.shape
    words = np.ascontiguousarray(words).reshape(g, 128, n, -1)
    if fmt == "e4m3":
        vals = words.view(ml_dtypes.float8_e4m3fn).astype(np.float64)
    else:
        nib = np.empty((g, 128, n, 4), np.uint8)
        nib[..., 0::2] = words & 0xF
        nib[..., 1::2] = words >> 4
        vals = E2M1[nib]
    vals = vals * np.repeat(np.exp2(scales.astype(np.float64) - 127.0), 8, axis=1)[..., None]
    return vals.transpose(0, 1, 3, 2).reshape(g * 512, n)


def gelu(v):
    return 0.5 * v * (1.0 + np.tanh(np.sqrt(2.0 / np.pi) * (v + 0.044715 * v**3)))


def bf(x):
    return np.asarray(x, np.float32).astype(ml_dtypes.bfloat16)


def planes(Y):
    n, m = Y.shape
    b = f64(bf(Y)).reshape(n // 32, 32, m)
    amax = np.abs(b).max(1)
    byte = np.clip(np.where(amax > 0, np.frexp(amax)[1] - 1 + 127 - 7, 1), 1, 254)
    codes = (b * np.exp2(127.0 - byte)[:, None, :]).reshape(n, m).astype(np.float32).astype(ml_dtypes.float8_e4m3fn).view(np.uint8)
    words = codes.reshape(n // 512, 128, 4, m).transpose(0, 1, 3, 2)
    return np.ascontiguousarray(words), np.ascontiguousarray(byte.astype(np.uint8).reshape(n // 512, 16, m))


K, H, N, T, S, P = 512, 1024, 512, 4096, 1024, 512

def setup_inputs():
    n = np.random.standard_normal
    s = mx_kscale(K)[:, None]
    u = mx_kscale(H)[:, None]
    tab_words, tab_scales = pack_weight(n((K, T)) * s, "e4m3")
    w2_words, w2_scales = pack_weight(1.3 * n((K, H)) / np.sqrt(K) / s, "e2m1")
    wa_words, wa_scales = pack_weight(n((H, N)) / np.sqrt(H) / u, "e4m3")
    return {
        "tab_words": tab_words, "tab_scales": tab_scales,
        "offs": striped(np.random.permutation(T)[:S]),
        "pos1": striped(np.random.permutation(S)[:P]),
        "pos2": striped(np.random.permutation(S)[:P]),
        "w1": (1.3 * n((K, H)) / np.sqrt(K) / s).astype(np.float32),
        "w2_words": w2_words, "w2_scales": w2_scales,
        "gain": (np.exp(0.3 * n(H)) * u[:, 0]).astype(np.float32),
        "oral": (0.7 + 0.7 * n((H, P))).astype(np.float32),
        "wa_words": wa_words, "wa_scales": wa_scales,
        "wb": (n((H, N)) / np.sqrt(H) / u).astype(np.float32),
        "bias": (0.8 * n(N)).astype(np.float32),
        "reader": (0.5 * np.exp(0.8 * n(N))[:, None] * np.exp(0.4 * n((N, P)))).astype(np.float32),
    }

def reference(tab_words, tab_scales, offs, pos1, pos2, w1, w2_words, w2_scales, gain, oral, wa_words, wa_scales, wb, bias, reader):
    v = unpack_weight(tab_words, tab_scales, "e4m3")[:, unstriped(offs)]
    w2 = unpack_weight(w2_words, w2_scales, "e2m1")
    wa = unpack_weight(wa_words, wa_scales, "e4m3")
    l1, l2 = unstriped(pos1), unstriped(pos2)
    top = np.maximum(mxq(f64(w1), 0, "e4m3").T @ v, w2.T @ v)
    h = top * f64(gain)[:, None]
    xa = h[:, l1] * f64(oral)
    xb = h[:, l2] * np.tanh(top[:, l2])
    e = wa.T @ mxq(xa, 0, "e4m3") + mxq(f64(wb), 0, "e4m3").T @ mxq(xb, 0, "e4m3")
    y = (e + f64(bias)[:, None]) * f64(reader)
    words, scales = planes(y)
    return y, words, scales

@@ -1,0 +1,286 @@
+from contextlib import ExitStack
+
+import concourse.mybir as mybir
+
+K, H, N, T, S, J = 512, 1024, 512, 4096, 1024, 512
+FLOPS = 2 * (2 * K * H * S + 2 * H * N * J)
+
+F32 = mybir.dt.float32
+BF16 = mybir.dt.bfloat16
+I32 = mybir.dt.int32
+U32 = mybir.dt.uint32
+U16 = mybir.dt.uint16
+U8 = mybir.dt.uint8
+FP8X4 = mybir.dt.float8_e4m3fn_x4
+FP4X4 = mybir.dt.float4_e2m1fn_x4
+ALU = mybir.AluOpType
+ACT = mybir.ActivationFunctionType
+
+P = 128
+PACK = 4
+GROUP = P * PACK
+BANK = 512
+LIST = 16
+CHUNKS = ((0, 256), (256, 384), (384, 512))
+
+
+def load_scale_rows(queues, plane, rows):
+    for quad, queue in enumerate(queues):
+        queue.dma_start(
+            out=plane[32 * quad : 32 * quad + 4, :].bitcast(I32),
+            in_=rows[4 * quad : 4 * quad + 4, :].bitcast(I32),
+        )
+
+
+def tile_list_swallow_phase_features_kernel(
+    tc, tab_words, tab_scales, offs, pos1, pos2, w1, w2_words, w2_scales, gain, oral,
+    wa_words, wa_scales, wb, bias, reader, out_0, out_1, out_2,
+):
+    nc = tc.nc
+    with ExitStack() as ctx:
+        keep = ctx.enter_context(tc.tile_pool(name="keep", bufs=1))
+        ring = ctx.enter_context(tc.tile_pool(name="ring", bufs=2))
+        psum = ctx.enter_context(tc.psum_pool(name="psum", bufs=1))
+
+        idx = keep.tile([P, S // LIST], U16, name="idx")
+        p1 = keep.tile([P, J // LIST], U16, name="p1")
+        p2 = keep.tile([P, J // LIST], U16, name="p2")
+
+        tabw = keep.tile([P, T], I32, name="tabw", tag="tabw_oral1", align_bytes=64)
+        tabs = keep.tile([P, T], U8, name="tabs", tag="tabs_oral0_reader", align_bytes=64)
+        w2w_raw = keep.tile([P, 2 * H], U8, name="w2w_raw", tag="w2w_waw", align_bytes=64)
+        w2s_raw = keep.tile([P, H], U8, name="w2s_raw", tag="w2s_was_bias", align_bytes=64)
+        gain_sb = keep.tile([P, 2, PACK], F32, name="gain_sb")
+
+        def load_weight(rows, name):
+            raw = ring.tile([P, PACK, GROUP], F32, name=name, tag="w_raw", bufs=1)
+            nc.sync.dma_start(out=raw[:], in_=rows.rearrange("(p i) c -> p i c", i=PACK))
+            return raw
+
+        def quantise_weight(raw, name):
+            dealt = ring.tile([P, PACK, P, PACK], BF16, name=name + "_bf", tag="w_bf", align_bytes=64)
+            nc.scalar.copy(
+                out=dealt[:].rearrange("p t q i -> p q t i"),
+                in_=raw[:].rearrange("p i (q t) -> p q t i", t=PACK),
+            )
+            codes = keep.tile([P, GROUP], U32, name=name + "_codes", align_bytes=64)
+            scales = keep.tile([P, GROUP], U8, name=name + "_scales", align_bytes=64)
+            nc.vector.quantize_mx(
+                out=codes[:].bitcast(FP8X4), scales=scales[:], in_=dealt[:].rearrange("p t q i -> p (t q i)")
+            )
+            return codes, scales
+
+        nc.vector.memset(tabs[:].bitcast(I32), 0)
+        nc.gpsimd.memset(w2s_raw[:].bitcast(I32), 0)
+        nc.sync.dma_start(idx[:], offs)
+        nc.scalar.dma_start(out=gain_sb[:], in_=gain.rearrange("(a p t) -> p a t", a=2, t=PACK))
+        nc.sync.dma_start(p2[:], pos2)
+        nc.sync.dma_start(p1[:], pos1)
+        nc.sync.dma_start(out=w2w_raw[:].bitcast(I32), in_=w2_words[0].bitcast(I32))
+        w1_raw0 = load_weight(w1[:, 0:GROUP], "w1_raw0")
+        nc.sync.dma_start(out=tabw[:], in_=tab_words[0].rearrange("p t i -> p (t i)").bitcast(I32))
+        load_scale_rows((nc.scalar,) * 4, tabs, tab_scales[0])
+        load_scale_rows((nc.scalar, nc.gpsimd) * 2, w2s_raw, w2_scales[0])
+
+        def load_rows(rows, name, tag):
+            dealt = keep.tile([P, PACK, J], F32, name=name, tag=tag, align_bytes=64)
+            nc.sync.dma_start(out=dealt[:], in_=rows.rearrange("(p t) j -> p t j", t=PACK))
+            return dealt
+
+        vs = keep.tile([P, S], U8, name="vs", align_bytes=64)
+        nc.vector.tensor_copy(out=vs[:], in_=tabs[:].indirect(idx[:]))
+        oral_sb = [load_rows(oral[0:GROUP, :], "oral0", "tabs_oral0_reader")]
+
+        def deal_w2(a):
+            words = keep.tile([P, PACK, P, 2], U8, name="w2w%d" % a, align_bytes=64)
+            nc.vector.tensor_copy(
+                out=words[:],
+                in_=w2w_raw[:, 2 * a * GROUP : 2 * (a + 1) * GROUP].rearrange("p (q t b) -> p t q b", t=PACK, b=2),
+            )
+            scales = keep.tile([P, PACK, P], U8, name="w2s%d" % a, align_bytes=64)
+            nc.vector.tensor_copy(
+                out=scales[:], in_=w2s_raw[:, a * GROUP : (a + 1) * GROUP].rearrange("p (q t) -> p t q", t=PACK)
+            )
+            return words, scales
+
+        w2q = [deal_w2(0)]
+        w1q = [quantise_weight(w1_raw0, "w1q0")]
+        w1_raw1 = load_weight(w1[:, GROUP : 2 * GROUP], "w1_raw1")
+        vw = []
+        for half in range(2):
+            words = keep.tile([P, BANK], U32, name="vw%d" % half, align_bytes=64)
+            cols = slice(half * BANK // LIST, (half + 1) * BANK // LIST)
+            nc.vector.tensor_copy(out=words[:], in_=tabw[:].bitcast(U32).indirect(idx[:, cols]))
+            vw.append(words)
+        oral_sb.append(load_rows(oral[GROUP : 2 * GROUP, :], "oral1", "tabw_oral1"))
+        w2q.append(deal_w2(1))
+        waw_raw = keep.tile([P, 2, N], I32, name="waw_raw", tag="w2w_waw", align_bytes=64)
+        nc.sync.dma_start(out=waw_raw[:], in_=wa_words.rearrange("a p n i -> p a (n i)").bitcast(I32))
+        was_raw = keep.tile([P, N], U8, name="was_raw", tag="w2s_was_bias", align_bytes=64)
+        nc.gpsimd.memset(was_raw[:].bitcast(I32), 0)
+        for quad in range(4):
+            nc.sync.dma_start(
+                out=was_raw[32 * quad : 32 * quad + 8, :].bitcast(I32),
+                in_=wa_scales[:, 4 * quad : 4 * quad + 4, :].bitcast(I32),
+            )
+
+        def first_stage(a, t):
+            top = ring.tile([P, S], F32, name="top%d%d" % (a, t), tag="top", bufs=5)
+            for half in range(2):
+                cols = slice(half * BANK, (half + 1) * BANK)
+                sum1 = psum.tile([P, BANK], F32, name="sum1", tag="sum1", bufs=2)
+                sum2 = psum.tile([P, BANK], F32, name="sum2", tag="sum2", bufs=2)
+                nc.tensor.matmul_mx(
+                    out=sum2[:],
+                    lhsT=w2q[a][0][:, t, :, :].rearrange("p q b -> p (q b)").bitcast(FP4X4),
+                    lhsT_scale=w2q[a][1][:, t, :],
+                    rhs=vw[half][:].bitcast(FP8X4), rhs_scale=vs[:, cols], start=True, stop=True,
+                )
+                nc.tensor.matmul_mx(
+                    out=sum1[:],
+                    lhsT=w1q[a][0][:, t * P : (t + 1) * P].bitcast(FP8X4),
+                    lhsT_scale=w1q[a][1][:, t * P : (t + 1) * P],
+                    rhs=vw[half][:].bitcast(FP8X4), rhs_scale=vs[:, cols], start=True, stop=True,
+                )
+                nc.scalar.copy(out=top[:, cols], in_=sum2[:])
+                nc.vector.tensor_tensor(out=top[:, cols], in0=sum1[:], in1=top[:, cols], op=ALU.max)
+            gained = oral_sb[a][:, t, :]
+            nc.scalar.activation(out=gained, in_=gained, func=ACT.Copy, scale=gain_sb[:, a, t : t + 1])
+            return top
+
+        def pick(a, t, top, lo, hi, xa, xb):
+            width = hi - lo
+            cols = slice(lo // LIST, hi // LIST)
+            picked = ring.tile([P, width], F32, name="picked", tag="picked", bufs=3)
+            nc.vector.tensor_copy(out=picked[:], in_=top[:].indirect(p2[:, cols]))
+            bent = ring.tile([P, width], F32, name="bent", tag="bent", bufs=3)
+            nc.scalar.activation(out=bent[:], in_=picked[:], func=ACT.Tanh)
+            nc.vector.tensor_tensor(
+                out=xa[:, t, :], in0=top[:].indirect(p1[:, cols]), in1=oral_sb[a][:, t, lo:hi], op=ALU.mult
+            )
+            nc.vector.scalar_tensor_tensor(
+                out=xb[:, t, :], in0=picked[:], scalar=gain_sb[:, a, t : t + 1], in1=bent[:],
+                op0=ALU.mult, op1=ALU.mult,
+            )
+
+        def weave(rows, width, name):
+            woven = ring.tile([P, width * PACK], BF16, name=name, tag="woven", bufs=3, align_bytes=64)
+            nc.scalar.copy(
+                out=woven[:].rearrange("p (c i t) -> p c t i", i=PACK, t=PACK),
+                in_=rows[:].rearrange("p t (c i) -> p c t i", i=PACK),
+            )
+            return woven
+
+        def quantise(woven, width, name):
+            codes = keep.tile([P, width], U32, name=name + "_codes", align_bytes=64)
+            scales = keep.tile([P, width], U8, name=name + "_scales", align_bytes=64)
+            nc.vector.quantize_mx(out=codes[:].bitcast(FP8X4), scales=scales[:], in_=woven[:])
+            return codes, scales
+
+        def x_tiles(width):
+            xa = ring.tile([P, PACK, width], F32, name="xa", tag="xa")
+            xb = ring.tile([P, PACK, width], BF16, name="xb", tag="xb")
+            return xa, xb
+
+        banks = []
+        for c, (lo, hi) in enumerate(CHUNKS):
+            per_bank = BANK // (hi - lo)
+            banks.append([
+                psum.tile([P, per_bank, hi - lo], F32, name="e%d%d" % (c, b)) for b in range(PACK // per_bank)
+            ])
+
+        def second_pass(c, weight, x, x_lo, first, last):
+            lo, hi = CHUNKS[c]
+            per_bank = BANK // (hi - lo)
+            cols = slice(lo - x_lo, hi - x_lo)
+            for t in range(PACK):
+                nc.tensor.matmul_mx(
+                    out=banks[c][t // per_bank][:, t % per_bank, :],
+                    lhsT=weight[0][:, t * P : (t + 1) * P].bitcast(FP8X4),
+                    lhsT_scale=weight[1][:, t * P : (t + 1) * P],
+                    rhs=x[0][:, cols].bitcast(FP8X4), rhs_scale=x[1][:, cols],
+                    start=first and t % per_bank == 0, stop=last and t % per_bank == per_bank - 1,
+                )
+
+        xa0, xb0 = x_tiles(J)
+        for t in range(PACK):
+            top = first_stage(0, t)
+            pick(0, t, top, 0, J, xa0, xb0)
+            if t == 1:
+                w1q.append(quantise_weight(w1_raw1, "w1q1"))
+                wb_raw0 = load_weight(wb[0:GROUP, :], "wb_raw0")
+            if t == 3:
+                wbq = [quantise_weight(wb_raw0, "wbq0")]
+                wb_raw1 = load_weight(wb[GROUP : 2 * GROUP, :], "wb_raw1")
+        reader_sb = load_rows(reader, "reader_sb", "tabs_oral0_reader")
+
+        tops = []
+        xa1, xb1 = x_tiles(CHUNKS[0][1])
+        waq = []
+        for t in range(PACK):
+            tops.append(first_stage(1, t))
+            pick(1, t, tops[t], CHUNKS[0][0], CHUNKS[0][1], xa1, xb1)
+            if t == 0:
+                xa0q = quantise(weave(xa0, J, "xa0w"), J, "xa0")
+                was = keep.tile([P, PACK, P], U8, name="was", align_bytes=64)
+                nc.vector.tensor_copy(out=was[:], in_=was_raw[:].rearrange("p (q t) -> p t q", t=PACK))
+                bias_sb = keep.tile([P, PACK], F32, name="bias_sb", tag="w2s_was_bias", align_bytes=64)
+                nc.sync.dma_start(out=bias_sb[:], in_=bias.rearrange("(p t) -> p t", t=PACK))
+                for a in range(2):
+                    words = keep.tile([P, PACK, P], I32, name="waw%d" % a, align_bytes=64)
+                    nc.vector.tensor_copy(out=words[:], in_=waw_raw[:, a, :].rearrange("p (q t) -> p t q", t=PACK))
+                    waq.append((
+                        words[:].rearrange("p t q -> p (t q)"), was[4 * a : P, :, :].rearrange("p t q -> p (t q)")
+                    ))
+            if t == 1:
+                xb0q = quantise(weave(xb0, J, "xb0w"), J, "xb0")
+            if t == 2:
+                wbq.append(quantise_weight(wb_raw1, "wbq1"))
+        for c in range(len(CHUNKS)):
+            second_pass(c, waq[0], xa0q, 0, True, False)
+            second_pass(c, wbq[0], xb0q, 0, False, False)
+
+        out_rows = out_0.rearrange("(p t) j -> p t j", t=PACK)
+        out_words = out_1[0].rearrange("p m t -> p (m t)").bitcast(I32)
+        y_codes = keep.tile([P, J], U32, name="y_codes", align_bytes=64)
+        y_scales = keep.tile([P, J], U8, name="y_scales", align_bytes=64)
+
+        def finish_products(c, xa, xb):
+            lo, hi = CHUNKS[c]
+            xaq = quantise(weave(xa, hi - lo, "xa1w"), hi - lo, "xa1%d" % c)
+            xbq = quantise(weave(xb, hi - lo, "xb1w"), hi - lo, "xb1%d" % c)
+            second_pass(c, waq[1], xaq, lo, False, False)
+            second_pass(c, wbq[1], xbq, lo, False, True)
+
+        def finish_output(c):
+            lo, hi = CHUNKS[c]
+            per_bank = BANK // (hi - lo)
+            y = keep.tile([P, PACK, hi - lo], F32, name="y%d" % c)
+            for t in range(PACK):
+                nc.vector.scalar_tensor_tensor(
+                    out=y[:, t, :], in0=banks[c][t // per_bank][:, t % per_bank, :], scalar=bias_sb[:, t : t + 1],
+                    in1=reader_sb[:, t, lo:hi], op0=ALU.add, op1=ALU.mult,
+                )
+            nc.sync.dma_start(out=out_rows[:, :, lo:hi], in_=y[:])
+            woven = weave(y, hi - lo, "yw")
+            nc.vector.quantize_mx(out=y_codes[:, lo:hi].bitcast(FP8X4), scales=y_scales[:, lo:hi], in_=woven[:])
+            nc.sync.dma_start(out=out_words[:, lo:hi], in_=y_codes[:, lo:hi].bitcast(I32))
+
+        waiting = (xa1, xb1)
+        for c in range(1, len(CHUNKS)):
+            lo, hi = CHUNKS[c]
+            xa, xb = x_tiles(hi - lo)
+            for t in range(PACK):
+                pick(1, t, tops[t], lo, hi, xa, xb)
+                if t == 1:
+                    finish_products(c - 1, waiting[0], waiting[1])
+            finish_output(c - 1)
+            waiting = (xa, xb)
+        finish_products(len(CHUNKS) - 1, waiting[0], waiting[1])
+        finish_output(len(CHUNKS) - 1)
+        for quad in range(4):
+            queue = nc.scalar if quad % 2 else nc.sync
+            queue.dma_start(
+                out=out_2[0, 4 * quad : 4 * quad + 4, :].bitcast(I32),
+                in_=y_scales[32 * quad : 32 * quad + 4, :].bitcast(I32),
+            )

@@ -21,15 +21,14 @@ PACK = 4
 GROUP = P * PACK
 BANK = 512
 LIST = 16
-CHUNKS = ((0, 256), (256, 384), (384, 512))
+CHUNKS = ((0, 256), (256, 512))
+PIECES = 4
+COUNTS = (0, 2, 3, 3, 3, 3, 3, 3)
 
 
 def load_scale_rows(queues, plane, rows):
-    for quad, queue in enumerate(queues):
-        queue.dma_start(
-            out=plane[32 * quad : 32 * quad + 4, :].bitcast(I32),
-            in_=rows[4 * quad : 4 * quad + 4, :].bitcast(I32),
-        )
+    for r, queue in enumerate(queues):
+        queue.dma_start(out=plane[r:P:32, :].bitcast(I32), in_=rows[r:16:4, :].bitcast(I32))
 
 
 def tile_list_swallow_phase_features_kernel(
@@ -46,74 +45,89 @@ def tile_list_swallow_phase_features_kernel(
         p1 = keep.tile([P, J // LIST], U16, name="p1")
         p2 = keep.tile([P, J // LIST], U16, name="p2")
 
-        tabw = keep.tile([P, T], I32, name="tabw", tag="tabw_oral1", align_bytes=64)
-        tabs = keep.tile([P, T], U8, name="tabs", tag="tabs_oral0_reader", align_bytes=64)
+        tabw = keep.tile([P, T], I32, name="tabw", tag="tabw_wb", align_bytes=64)
+        tabs = keep.tile([P, T], U8, name="tabs", tag="tabs_w1_oral", align_bytes=64)
         w2w_raw = keep.tile([P, 2 * H], U8, name="w2w_raw", tag="w2w_waw", align_bytes=64)
         w2s_raw = keep.tile([P, H], U8, name="w2s_raw", tag="w2s_was_bias", align_bytes=64)
         gain_sb = keep.tile([P, 2, PACK], F32, name="gain_sb")
 
-        def load_weight(rows, name):
-            raw = ring.tile([P, PACK, GROUP], F32, name=name, tag="w_raw", bufs=1)
-            nc.sync.dma_start(out=raw[:], in_=rows.rearrange("(p i) c -> p i c", i=PACK))
-            return raw
-
-        def quantise_weight(raw, name):
-            dealt = ring.tile([P, PACK, P, PACK], BF16, name=name + "_bf", tag="w_bf", align_bytes=64)
-            nc.scalar.copy(
-                out=dealt[:].rearrange("p t q i -> p q t i"),
-                in_=raw[:].rearrange("p i (q t) -> p q t i", t=PACK),
-            )
-            codes = keep.tile([P, GROUP], U32, name=name + "_codes", align_bytes=64)
-            scales = keep.tile([P, GROUP], U8, name=name + "_scales", align_bytes=64)
-            nc.vector.quantize_mx(
-                out=codes[:].bitcast(FP8X4), scales=scales[:], in_=dealt[:].rearrange("p t q i -> p (t q i)")
-            )
-            return codes, scales
-
-        nc.vector.memset(tabs[:].bitcast(I32), 0)
-        nc.gpsimd.memset(w2s_raw[:].bitcast(I32), 0)
-        nc.sync.dma_start(idx[:], offs)
-        nc.scalar.dma_start(out=gain_sb[:], in_=gain.rearrange("(a p t) -> p a t", a=2, t=PACK))
-        nc.sync.dma_start(p2[:], pos2)
-        nc.sync.dma_start(p1[:], pos1)
-        nc.sync.dma_start(out=w2w_raw[:].bitcast(I32), in_=w2_words[0].bitcast(I32))
-        w1_raw0 = load_weight(w1[:, 0:GROUP], "w1_raw0")
-        nc.sync.dma_start(out=tabw[:], in_=tab_words[0].rearrange("p t i -> p (t i)").bitcast(I32))
-        load_scale_rows((nc.scalar,) * 4, tabs, tab_scales[0])
-        load_scale_rows((nc.scalar, nc.gpsimd) * 2, w2s_raw, w2_scales[0])
-
         def load_rows(rows, name, tag):
-            dealt = keep.tile([P, PACK, J], F32, name=name, tag=tag, align_bytes=64)
+            dealt = keep.tile([P, PACK, GROUP], F32, name=name, tag=tag, align_bytes=64)
             nc.sync.dma_start(out=dealt[:], in_=rows.rearrange("(p t) j -> p t j", t=PACK))
             return dealt
 
-        vs = keep.tile([P, S], U8, name="vs", align_bytes=64)
-        nc.vector.tensor_copy(out=vs[:], in_=tabs[:].indirect(idx[:]))
-        oral_sb = [load_rows(oral[0:GROUP, :], "oral0", "tabs_oral0_reader")]
+        def quantise(woven, width, name):
+            codes = keep.tile([P, width], U32, name=name + "_codes", align_bytes=64)
+            scales = keep.tile([P, width], U8, name=name + "_scales", align_bytes=64)
+            nc.vector.quantize_mx(out=codes[:].bitcast(FP8X4), scales=scales[:], in_=woven[:])
+            return codes, scales
 
-        def deal_w2(a):
+        def woven_tile(width):
+            return ring.tile([P, width * PACK], BF16, name="woven", tag="woven", bufs=5, align_bytes=64)
+
+        def deal_weight(woven, raw, piece, pieces):
+            part = slice(piece * P // pieces, (piece + 1) * P // pieces)
+            nc.scalar.copy(
+                out=woven[:].rearrange("p (t q i) -> p q t i", t=PACK, i=PACK)[:, part, :, :],
+                in_=raw.rearrange("p i (q t) -> p q t i", t=PACK)[:, part, :, :],
+            )
+
+        def weave(woven, rows, lo, hi):
+            nc.scalar.copy(
+                out=woven[:, lo * PACK : hi * PACK].rearrange("p (c i t) -> p c t i", i=PACK, t=PACK),
+                in_=rows[:, :, lo:hi].rearrange("p t (c i) -> p c t i", i=PACK),
+            )
+
+        def quantise_weight(raw, name, pieces):
+            woven = woven_tile(GROUP)
+            for piece in range(pieces):
+                deal_weight(woven, raw, piece, pieces)
+            return quantise(woven, GROUP, name)
+
+        nc.gpsimd.memset(w2s_raw[:].bitcast(I32), 0)
+        nc.vector.memset(tabs[:].bitcast(I32), 0)
+        nc.sync.dma_start(out=w2w_raw[:].bitcast(I32), in_=w2_words[0].bitcast(I32))
+        nc.sync.dma_start(idx[:], offs)
+        load_scale_rows((nc.sync,) * 4, w2s_raw, w2_scales[0])
+        w1_raw0 = load_rows(w1[:, 0:GROUP], "w1_raw0", "w1_oral_reader")
+        load_scale_rows((nc.sync,) * 4, tabs, tab_scales[0])
+        nc.sync.dma_start(out=tabw[:], in_=tab_words[0].rearrange("p t i -> p (t i)").bitcast(I32))
+        nc.sync.dma_start(p2[:], pos2)
+        nc.sync.dma_start(p1[:], pos1)
+        nc.sync.dma_start(out=gain_sb[:], in_=gain.rearrange("(a p t) -> p a t", a=2, t=PACK))
+
+        def deal_w2_words(a):
             words = keep.tile([P, PACK, P, 2], U8, name="w2w%d" % a, align_bytes=64)
             nc.vector.tensor_copy(
                 out=words[:],
                 in_=w2w_raw[:, 2 * a * GROUP : 2 * (a + 1) * GROUP].rearrange("p (q t b) -> p t q b", t=PACK, b=2),
             )
-            scales = keep.tile([P, PACK, P], U8, name="w2s%d" % a, align_bytes=64)
-            nc.vector.tensor_copy(
-                out=scales[:], in_=w2s_raw[:, a * GROUP : (a + 1) * GROUP].rearrange("p (q t) -> p t q", t=PACK)
-            )
-            return words, scales
+            return words
 
-        w2q = [deal_w2(0)]
-        w1q = [quantise_weight(w1_raw0, "w1q0")]
-        w1_raw1 = load_weight(w1[:, GROUP : 2 * GROUP], "w1_raw1")
+        def deal_bytes(raw, name):
+            scales = keep.tile([P, PACK, P], U8, name=name, align_bytes=64)
+            nc.vector.tensor_copy(out=scales[:], in_=raw.rearrange("p (q t) -> p t q", t=PACK))
+            return scales
+
+        w2w = [deal_w2_words(0), deal_w2_words(1)]
+        w2s = [deal_bytes(w2s_raw[:, a * GROUP : (a + 1) * GROUP], "w2s%d" % a) for a in range(2)]
+        vs = keep.tile([P, S], U8, name="vs", align_bytes=64)
+        nc.vector.tensor_copy(out=vs[:], in_=tabs[:].indirect(idx[:]))
+        w1q = [quantise_weight(w1_raw0[:], "w1q0", 1)]
+        oral_sb = [load_rows(oral[0:GROUP, :], "oral0", "w1_oral_reader")]
+        w1_raw1 = load_rows(w1[:, GROUP : 2 * GROUP], "w1_raw1", "tabs_w1_oral")
         vw = []
         for half in range(2):
             words = keep.tile([P, BANK], U32, name="vw%d" % half, align_bytes=64)
             cols = slice(half * BANK // LIST, (half + 1) * BANK // LIST)
             nc.vector.tensor_copy(out=words[:], in_=tabw[:].bitcast(U32).indirect(idx[:, cols]))
             vw.append(words)
-        oral_sb.append(load_rows(oral[GROUP : 2 * GROUP, :], "oral1", "tabw_oral1"))
-        w2q.append(deal_w2(1))
+
+        wb_raw = keep.tile([P, 2, PACK, N], F32, name="wb_raw", tag="tabw_wb", align_bytes=64)
+        for a in range(2):
+            nc.sync.dma_start(
+                out=wb_raw[:, a, :, :], in_=wb[a * GROUP : (a + 1) * GROUP, :].rearrange("(p i) n -> p i n", i=PACK)
+            )
         waw_raw = keep.tile([P, 2, N], I32, name="waw_raw", tag="w2w_waw", align_bytes=64)
         nc.sync.dma_start(out=waw_raw[:], in_=wa_words.rearrange("a p n i -> p a (n i)").bitcast(I32))
         was_raw = keep.tile([P, N], U8, name="was_raw", tag="w2s_was_bias", align_bytes=64)
@@ -125,15 +139,15 @@ def tile_list_swallow_phase_features_kernel(
             )
 
         def first_stage(a, t):
-            top = ring.tile([P, S], F32, name="top%d%d" % (a, t), tag="top", bufs=5)
+            top = ring.tile([P, S], F32, name="top%d%d" % (a, t), tag="top", bufs=6)
             for half in range(2):
                 cols = slice(half * BANK, (half + 1) * BANK)
                 sum1 = psum.tile([P, BANK], F32, name="sum1", tag="sum1", bufs=2)
                 sum2 = psum.tile([P, BANK], F32, name="sum2", tag="sum2", bufs=2)
                 nc.tensor.matmul_mx(
                     out=sum2[:],
-                    lhsT=w2q[a][0][:, t, :, :].rearrange("p q b -> p (q b)").bitcast(FP4X4),
-                    lhsT_scale=w2q[a][1][:, t, :],
+                    lhsT=w2w[a][:, t, :, :].rearrange("p q b -> p (q b)").bitcast(FP4X4),
+                    lhsT_scale=w2s[a][:, t, :],
                     rhs=vw[half][:].bitcast(FP8X4), rhs_scale=vs[:, cols], start=True, stop=True,
                 )
                 nc.tensor.matmul_mx(
@@ -148,7 +162,7 @@ def tile_list_swallow_phase_features_kernel(
             nc.scalar.activation(out=gained, in_=gained, func=ACT.Copy, scale=gain_sb[:, a, t : t + 1])
             return top
 
-        def pick(a, t, top, lo, hi, xa, xb):
+        def pick(a, t, top, lo, hi, xa):
             width = hi - lo
             cols = slice(lo // LIST, hi // LIST)
             picked = ring.tile([P, width], F32, name="picked", tag="picked", bufs=3)
@@ -158,24 +172,13 @@ def tile_list_swallow_phase_features_kernel(
             nc.vector.tensor_tensor(
                 out=xa[:, t, :], in0=top[:].indirect(p1[:, cols]), in1=oral_sb[a][:, t, lo:hi], op=ALU.mult
             )
+            return picked, bent
+
+        def bend(a, t, pair, xb):
             nc.vector.scalar_tensor_tensor(
-                out=xb[:, t, :], in0=picked[:], scalar=gain_sb[:, a, t : t + 1], in1=bent[:],
+                out=xb[:, t, :], in0=pair[0][:], scalar=gain_sb[:, a, t : t + 1], in1=pair[1][:],
                 op0=ALU.mult, op1=ALU.mult,
             )
-
-        def weave(rows, width, name):
-            woven = ring.tile([P, width * PACK], BF16, name=name, tag="woven", bufs=3, align_bytes=64)
-            nc.scalar.copy(
-                out=woven[:].rearrange("p (c i t) -> p c t i", i=PACK, t=PACK),
-                in_=rows[:].rearrange("p t (c i) -> p c t i", i=PACK),
-            )
-            return woven
-
-        def quantise(woven, width, name):
-            codes = keep.tile([P, width], U32, name=name + "_codes", align_bytes=64)
-            scales = keep.tile([P, width], U8, name=name + "_scales", align_bytes=64)
-            nc.vector.quantize_mx(out=codes[:].bitcast(FP8X4), scales=scales[:], in_=woven[:])
-            return codes, scales
 
         def x_tiles(width):
             xa = ring.tile([P, PACK, width], F32, name="xa", tag="xa")
@@ -202,55 +205,84 @@ def tile_list_swallow_phase_features_kernel(
                     start=first and t % per_bank == 0, stop=last and t % per_bank == per_bank - 1,
                 )
 
-        xa0, xb0 = x_tiles(J)
-        for t in range(PACK):
-            top = first_stage(0, t)
-            pick(0, t, top, 0, J, xa0, xb0)
-            if t == 1:
-                w1q.append(quantise_weight(w1_raw1, "w1q1"))
-                wb_raw0 = load_weight(wb[0:GROUP, :], "wb_raw0")
-            if t == 3:
-                wbq = [quantise_weight(wb_raw0, "wbq0")]
-                wb_raw1 = load_weight(wb[GROUP : 2 * GROUP, :], "wb_raw1")
-        reader_sb = load_rows(reader, "reader_sb", "tabs_oral0_reader")
+        xs0 = x_tiles(J)
+        xs1 = x_tiles(CHUNKS[0][1])
+        long_copies = []
+        made = {}
 
-        tops = []
-        xa1, xb1 = x_tiles(CHUNKS[0][1])
+        def plan(name, copy_piece):
+            woven = woven_tile(GROUP)
+            for piece in range(PIECES):
+                long_copies.append((name, woven, copy_piece, piece))
+
+        def run_long_copies(count):
+            for name, woven, copy_piece, piece in long_copies[:count]:
+                copy_piece(woven, piece)
+                if piece == PIECES - 1:
+                    made[name] = quantise(woven, GROUP, name)
+            del_count = long_copies[count:]
+            long_copies.clear()
+            long_copies.extend(del_count)
+
+        def weight_piece(raw):
+            return lambda woven, piece: deal_weight(woven, raw, piece, PIECES)
+
+        def rows_piece(rows):
+            return lambda woven, piece: weave(woven, rows, piece * J // PIECES, (piece + 1) * J // PIECES)
+
+        plan("w1q1", weight_piece(w1_raw1[:]))
+        plan("wbq0", weight_piece(wb_raw[:, 0, :, :]))
+        plan("wbq1", weight_piece(wb_raw[:, 1, :, :]))
+        counts = COUNTS
+        tops = [first_stage(0, 0)]
         waq = []
-        for t in range(PACK):
-            tops.append(first_stage(1, t))
-            pick(1, t, tops[t], CHUNKS[0][0], CHUNKS[0][1], xa1, xb1)
-            if t == 0:
-                xa0q = quantise(weave(xa0, J, "xa0w"), J, "xa0")
-                was = keep.tile([P, PACK, P], U8, name="was", align_bytes=64)
-                nc.vector.tensor_copy(out=was[:], in_=was_raw[:].rearrange("p (q t) -> p t q", t=PACK))
+        pair = None
+        for s in range(2 * PACK):
+            a, t = divmod(s, PACK)
+            if s + 1 < 2 * PACK:
+                tops.append(first_stage(*divmod(s + 1, PACK)))
+            if s > 0:
+                bend((s - 1) // PACK, (s - 1) % PACK, pair, (xs0, xs1)[(s - 1) // PACK][1])
+            pair = pick(a, t, tops[s], 0, (J, CHUNKS[0][1])[a], (xs0, xs1)[a][0])
+            if s == PACK:
+                plan("xa0", rows_piece(xs0[0]))
+                plan("xb0", rows_piece(xs0[1]))
+            run_long_copies(counts[s])
+            if s == 2:
+                w1q.append(made["w1q1"])
+                oral_sb.append(load_rows(oral[GROUP : 2 * GROUP, :], "oral1", "tabs_w1_oral"))
+            if s == PACK - 1:
+                reader_sb = load_rows(reader, "reader_sb", "w1_oral_reader")
+            if s == PACK:
+                was = deal_bytes(was_raw[:], "was")
                 bias_sb = keep.tile([P, PACK], F32, name="bias_sb", tag="w2s_was_bias", align_bytes=64)
                 nc.sync.dma_start(out=bias_sb[:], in_=bias.rearrange("(p t) -> p t", t=PACK))
-                for a in range(2):
-                    words = keep.tile([P, PACK, P], I32, name="waw%d" % a, align_bytes=64)
-                    nc.vector.tensor_copy(out=words[:], in_=waw_raw[:, a, :].rearrange("p (q t) -> p t q", t=PACK))
+                for g in range(2):
+                    words = keep.tile([P, PACK, P], I32, name="waw%d" % g, align_bytes=64)
+                    nc.vector.tensor_copy(out=words[:], in_=waw_raw[:, g, :].rearrange("p (q t) -> p t q", t=PACK))
                     waq.append((
-                        words[:].rearrange("p t q -> p (t q)"), was[4 * a : P, :, :].rearrange("p t q -> p (t q)")
+                        words[:].rearrange("p t q -> p (t q)"), was[4 * g : P, :, :].rearrange("p t q -> p (t q)")
                     ))
-            if t == 1:
-                xb0q = quantise(weave(xb0, J, "xb0w"), J, "xb0")
-            if t == 2:
-                wbq.append(quantise_weight(wb_raw1, "wbq1"))
+        bend(1, PACK - 1, pair, xs1[1])
+        wbq = [made["wbq0"], made["wbq1"]]
+        x0q = [made["xa0"], made["xb0"]]
+        tops = tops[PACK:]
+        xa1, xb1 = xs1
         for c in range(len(CHUNKS)):
-            second_pass(c, waq[0], xa0q, 0, True, False)
-            second_pass(c, wbq[0], xb0q, 0, False, False)
+            second_pass(c, waq[0], x0q[0], 0, True, False)
+            second_pass(c, wbq[0], x0q[1], 0, False, False)
 
         out_rows = out_0.rearrange("(p t) j -> p t j", t=PACK)
         out_words = out_1[0].rearrange("p m t -> p (m t)").bitcast(I32)
         y_codes = keep.tile([P, J], U32, name="y_codes", align_bytes=64)
         y_scales = keep.tile([P, J], U8, name="y_scales", align_bytes=64)
 
-        def finish_products(c, xa, xb):
+        def finish_products(c, xs):
             lo, hi = CHUNKS[c]
-            xaq = quantise(weave(xa, hi - lo, "xa1w"), hi - lo, "xa1%d" % c)
-            xbq = quantise(weave(xb, hi - lo, "xb1w"), hi - lo, "xb1%d" % c)
-            second_pass(c, waq[1], xaq, lo, False, False)
-            second_pass(c, wbq[1], xbq, lo, False, True)
+            for x, weight, last in ((xs[0], waq[1], False), (xs[1], wbq[1], True)):
+                woven = woven_tile(hi - lo)
+                weave(woven, x, 0, hi - lo)
+                second_pass(c, weight, quantise(woven, hi - lo, "x1q%d%d" % (c, last)), lo, False, last)
 
         def finish_output(c):
             lo, hi = CHUNKS[c]
@@ -262,7 +294,8 @@ def tile_list_swallow_phase_features_kernel(
                     in1=reader_sb[:, t, lo:hi], op0=ALU.add, op1=ALU.mult,
                 )
             nc.sync.dma_start(out=out_rows[:, :, lo:hi], in_=y[:])
-            woven = weave(y, hi - lo, "yw")
+            woven = woven_tile(hi - lo)
+            weave(woven, y, 0, hi - lo)
             nc.vector.quantize_mx(out=y_codes[:, lo:hi].bitcast(FP8X4), scales=y_scales[:, lo:hi], in_=woven[:])
             nc.sync.dma_start(out=out_words[:, lo:hi], in_=y_codes[:, lo:hi].bitcast(I32))
 
@@ -271,16 +304,17 @@ def tile_list_swallow_phase_features_kernel(
             lo, hi = CHUNKS[c]
             xa, xb = x_tiles(hi - lo)
             for t in range(PACK):
-                pick(1, t, tops[t], lo, hi, xa, xb)
+                fresh = pick(1, t, tops[t], lo, hi, xa)
+                if t > 0:
+                    bend(1, t - 1, pair, xb)
+                pair = fresh
                 if t == 1:
-                    finish_products(c - 1, waiting[0], waiting[1])
+                    finish_products(c - 1, waiting)
+            bend(1, PACK - 1, pair, xb)
             finish_output(c - 1)
             waiting = (xa, xb)
-        finish_products(len(CHUNKS) - 1, waiting[0], waiting[1])
+        finish_products(len(CHUNKS) - 1, waiting)
         finish_output(len(CHUNKS) - 1)
-        for quad in range(4):
-            queue = nc.scalar if quad % 2 else nc.sync
-            queue.dma_start(
-                out=out_2[0, 4 * quad : 4 * quad + 4, :].bitcast(I32),
-                in_=y_scales[32 * quad : 32 * quad + 4, :].bitcast(I32),
-            )
+        for r in range(4):
+            queue = nc.scalar if r % 2 else nc.sync
+            queue.dma_start(out=out_2[0, r:16:4, :].bitcast(I32), in_=y_scales[r:P:32, :].bitcast(I32))

@@ -23,6 +23,7 @@ BANK = 512
 LIST = 16
 CHUNKS = ((0, 256), (256, 512))
 PIECES = 4
+SCALAR_SHARE = 3
 COUNTS = (0, 2, 3, 3, 3, 3, 3, 3)
 
 
@@ -46,7 +47,7 @@ def tile_list_swallow_phase_features_kernel(
         p2 = keep.tile([P, J // LIST], U16, name="p2")
 
         tabw = keep.tile([P, T], I32, name="tabw", tag="tabw_wb", align_bytes=64)
-        tabs = keep.tile([P, T], U8, name="tabs", tag="tabs_w1_oral", align_bytes=64)
+        tabs = keep.tile([P, T], U8, name="tabs", align_bytes=64)
         w2w_raw = keep.tile([P, 2 * H], U8, name="w2w_raw", tag="w2w_waw", align_bytes=64)
         w2s_raw = keep.tile([P, H], U8, name="w2s_raw", tag="w2s_was_bias", align_bytes=64)
         gain_sb = keep.tile([P, 2, PACK], F32, name="gain_sb")
@@ -72,8 +73,8 @@ def tile_list_swallow_phase_features_kernel(
                 in_=raw.rearrange("p i (q t) -> p q t i", t=PACK)[:, part, :, :],
             )
 
-        def weave(woven, rows, lo, hi):
-            nc.scalar.copy(
+        def weave(woven, rows, lo, hi, copy_op=nc.scalar.copy):
+            copy_op(
                 out=woven[:, lo * PACK : hi * PACK].rearrange("p (c i t) -> p c t i", i=PACK, t=PACK),
                 in_=rows[:, :, lo:hi].rearrange("p t (c i) -> p c t i", i=PACK),
             )
@@ -84,17 +85,16 @@ def tile_list_swallow_phase_features_kernel(
                 deal_weight(woven, raw, piece, pieces)
             return quantise(woven, GROUP, name)
 
-        nc.gpsimd.memset(w2s_raw[:].bitcast(I32), 0)
-        nc.vector.memset(tabs[:].bitcast(I32), 0)
+        nc.gpsimd.memset(tabs[:].bitcast(I32), 0)
+        nc.vector.memset(w2s_raw[:].bitcast(I32), 0)
+        vs = keep.tile([P, S], U8, name="vs", align_bytes=64)
+        nc.vector.memset(vs[:].bitcast(I32), 0)
         nc.sync.dma_start(out=w2w_raw[:].bitcast(I32), in_=w2_words[0].bitcast(I32))
         nc.sync.dma_start(idx[:], offs)
         load_scale_rows((nc.sync,) * 4, w2s_raw, w2_scales[0])
+        nc.sync.dma_start(out=tabs[0:P:8, :].bitcast(I32), in_=tab_scales[0].bitcast(I32))
         w1_raw0 = load_rows(w1[:, 0:GROUP], "w1_raw0", "w1_oral_reader")
-        load_scale_rows((nc.sync,) * 4, tabs, tab_scales[0])
         nc.sync.dma_start(out=tabw[:], in_=tab_words[0].rearrange("p t i -> p (t i)").bitcast(I32))
-        nc.sync.dma_start(p2[:], pos2)
-        nc.sync.dma_start(p1[:], pos1)
-        nc.sync.dma_start(out=gain_sb[:], in_=gain.rearrange("(a p t) -> p a t", a=2, t=PACK))
 
         def deal_w2_words(a):
             words = keep.tile([P, PACK, P, 2], U8, name="w2w%d" % a, align_bytes=64)
@@ -109,12 +109,17 @@ def tile_list_swallow_phase_features_kernel(
             nc.vector.tensor_copy(out=scales[:], in_=raw.rearrange("p (q t) -> p t q", t=PACK))
             return scales
 
+        spread = keep.tile([P, S], U8, name="spread", tag="tabs_w1_oral", align_bytes=64)
+        nc.vector.tensor_copy(out=spread[:], in_=tabs[:].indirect(idx[:]))
+        for r in range(4):
+            nc.sync.dma_start(out=vs[r:P:32, :].bitcast(I32), in_=spread[8 * r : P : 32, :].bitcast(I32))
+        nc.sync.dma_start(p2[:], pos2)
+        nc.sync.dma_start(out=gain_sb[:], in_=gain.rearrange("(a p t) -> p a t", a=2, t=PACK))
         w2w = [deal_w2_words(0), deal_w2_words(1)]
         w2s = [deal_bytes(w2s_raw[:, a * GROUP : (a + 1) * GROUP], "w2s%d" % a) for a in range(2)]
-        vs = keep.tile([P, S], U8, name="vs", align_bytes=64)
-        nc.vector.tensor_copy(out=vs[:], in_=tabs[:].indirect(idx[:]))
         w1q = [quantise_weight(w1_raw0[:], "w1q0", 1)]
         oral_sb = [load_rows(oral[0:GROUP, :], "oral0", "w1_oral_reader")]
+        nc.sync.dma_start(p1[:], pos1)
         w1_raw1 = load_rows(w1[:, GROUP : 2 * GROUP], "w1_raw1", "tabs_w1_oral")
         vw = []
         for half in range(2):
@@ -167,16 +172,16 @@ def tile_list_swallow_phase_features_kernel(
             cols = slice(lo // LIST, hi // LIST)
             picked = ring.tile([P, width], F32, name="picked", tag="picked", bufs=3)
             nc.vector.tensor_copy(out=picked[:], in_=top[:].indirect(p2[:, cols]))
-            bent = ring.tile([P, width], F32, name="bent", tag="bent", bufs=3)
+            bent = ring.tile([P, width], F32, name="bent", tag="bent", bufs=4)
             nc.scalar.activation(out=bent[:], in_=picked[:], func=ACT.Tanh)
             nc.vector.tensor_tensor(
                 out=xa[:, t, :], in0=top[:].indirect(p1[:, cols]), in1=oral_sb[a][:, t, lo:hi], op=ALU.mult
             )
-            return picked, bent
+            return picked[:], bent
 
         def bend(a, t, pair, xb):
             nc.vector.scalar_tensor_tensor(
-                out=xb[:, t, :], in0=pair[0][:], scalar=gain_sb[:, a, t : t + 1], in1=pair[1][:],
+                out=xb[:, t, :], in0=pair[0], scalar=gain_sb[:, a, t : t + 1], in1=pair[1][:],
                 op0=ALU.mult, op1=ALU.mult,
             )
 
@@ -232,7 +237,6 @@ def tile_list_swallow_phase_features_kernel(
 
         plan("w1q1", weight_piece(w1_raw1[:]))
         plan("wbq0", weight_piece(wb_raw[:, 0, :, :]))
-        plan("wbq1", weight_piece(wb_raw[:, 1, :, :]))
         counts = COUNTS
         tops = [first_stage(0, 0)]
         waq = []
@@ -247,6 +251,7 @@ def tile_list_swallow_phase_features_kernel(
             if s == PACK:
                 plan("xa0", rows_piece(xs0[0]))
                 plan("xb0", rows_piece(xs0[1]))
+                plan("wbq1", weight_piece(wb_raw[:, 1, :, :]))
             run_long_copies(counts[s])
             if s == 2:
                 w1q.append(made["w1q1"])
@@ -277,14 +282,21 @@ def tile_list_swallow_phase_features_kernel(
         y_codes = keep.tile([P, J], U32, name="y_codes", align_bytes=64)
         y_scales = keep.tile([P, J], U8, name="y_scales", align_bytes=64)
 
-        def finish_products(c, xs):
-            lo, hi = CHUNKS[c]
-            for x, weight, last in ((xs[0], waq[1], False), (xs[1], wbq[1], True)):
-                woven = woven_tile(hi - lo)
-                weave(woven, x, 0, hi - lo)
-                second_pass(c, weight, quantise(woven, hi - lo, "x1q%d%d" % (c, last)), lo, False, last)
+        def shared_weave(woven, rows, width):
+            cut = width * SCALAR_SHARE // 8
+            weave(woven, rows, 0, cut)
+            weave(woven, rows, cut, width, nc.vector.tensor_copy)
 
-        def finish_output(c):
+        def product(c, x, weight, last, shared):
+            lo, hi = CHUNKS[c]
+            woven = woven_tile(hi - lo)
+            if shared:
+                shared_weave(woven, x, hi - lo)
+            else:
+                weave(woven, x, 0, hi - lo)
+            second_pass(c, weight, quantise(woven, hi - lo, "x1q%d%d" % (c, last)), lo, False, last)
+
+        def finish_output(c, shared):
             lo, hi = CHUNKS[c]
             per_bank = BANK // (hi - lo)
             y = keep.tile([P, PACK, hi - lo], F32, name="y%d" % c)
@@ -295,26 +307,39 @@ def tile_list_swallow_phase_features_kernel(
                 )
             nc.sync.dma_start(out=out_rows[:, :, lo:hi], in_=y[:])
             woven = woven_tile(hi - lo)
-            weave(woven, y, 0, hi - lo)
+            if shared:
+                shared_weave(woven, y, hi - lo)
+            else:
+                weave(woven, y, 0, hi - lo)
             nc.vector.quantize_mx(out=y_codes[:, lo:hi].bitcast(FP8X4), scales=y_scales[:, lo:hi], in_=woven[:])
             nc.sync.dma_start(out=out_words[:, lo:hi], in_=y_codes[:, lo:hi].bitcast(I32))
 
-        waiting = (xa1, xb1)
-        for c in range(1, len(CHUNKS)):
-            lo, hi = CHUNKS[c]
-            xa, xb = x_tiles(hi - lo)
-            for t in range(PACK):
-                fresh = pick(1, t, tops[t], lo, hi, xa)
-                if t > 0:
-                    bend(1, t - 1, pair, xb)
-                pair = fresh
-                if t == 1:
-                    finish_products(c - 1, waiting)
-            bend(1, PACK - 1, pair, xb)
-            finish_output(c - 1)
-            waiting = (xa, xb)
-        finish_products(len(CHUNKS) - 1, waiting)
-        finish_output(len(CHUNKS) - 1)
+        lo, hi = CHUNKS[1]
+        late = keep.tile([P, 2, PACK, hi - lo], F32, name="late", tag="tabw_wb", align_bytes=64)
+        xb = ring.tile([P, PACK, hi - lo], BF16, name="xb", tag="xb")
+        cols = slice(lo // LIST, hi // LIST)
+        pairs = []
+        for t in range(PACK):
+            nc.vector.tensor_copy(out=late[:, 1, t, :], in_=tops[t][:].indirect(p2[:, cols]))
+            bent = ring.tile([P, hi - lo], F32, name="bent", tag="bent", bufs=4)
+            nc.scalar.activation(out=bent[:], in_=late[:, 1, t, :], func=ACT.Tanh)
+            pairs.append((late[:, 1, t, :], bent))
+            if t == 1:
+                product(0, xa1, waq[1], False, False)
+            if t == 3:
+                product(0, xb1, wbq[1], True, False)
+        for t in range(PACK):
+            bend(1, t, pairs[t], xb)
+        for t in range(PACK):
+            nc.vector.tensor_tensor(
+                out=late[:, 0, t, :], in0=tops[t][:].indirect(p1[:, cols]), in1=oral_sb[1][:, t, lo:hi], op=ALU.mult
+            )
+            if t == 0:
+                product(1, xb, wbq[1], False, False)
+            if t == 1:
+                finish_output(0, False)
+        product(1, late[:, 0, :, :], waq[1], True, True)
+        finish_output(1, True)
         for r in range(4):
             queue = nc.scalar if r % 2 else nc.sync
             queue.dma_start(out=out_2[0, r:16:4, :].bitcast(I32), in_=y_scales[r:P:32, :].bitcast(I32))

@@ -24,7 +24,7 @@ LIST = 16
 CHUNKS = ((0, 256), (256, 512))
 PIECES = 4
 SCALAR_SHARE = 3
-COUNTS = (0, 2, 3, 3, 3, 3, 3, 3)
+COUNTS = (2, 3, 3, 3, 3, 2, 2, 2)
 
 
 def load_scale_rows(queues, plane, rows):
@@ -48,8 +48,8 @@ def tile_list_swallow_phase_features_kernel(
 
         tabw = keep.tile([P, T], I32, name="tabw", tag="tabw_wb", align_bytes=64)
         tabs = keep.tile([P, T], U8, name="tabs", align_bytes=64)
-        w2w_raw = keep.tile([P, 2 * H], U8, name="w2w_raw", tag="w2w_waw", align_bytes=64)
-        w2s_raw = keep.tile([P, H], U8, name="w2s_raw", tag="w2s_was_bias", align_bytes=64)
+        w2w_raw = keep.tile([P, 2 * H], U8, name="w2w_raw", align_bytes=64)
+        w2s_raw = keep.tile([P, H], U8, name="w2s_raw", align_bytes=64)
         gain_sb = keep.tile([P, 2, PACK], F32, name="gain_sb")
 
         def load_rows(rows, name, tag):
@@ -67,10 +67,11 @@ def tile_list_swallow_phase_features_kernel(
             return ring.tile([P, width * PACK], BF16, name="woven", tag="woven", bufs=5, align_bytes=64)
 
         def deal_weight(woven, raw, piece, pieces):
-            part = slice(piece * P // pieces, (piece + 1) * P // pieces)
+            pair, half = divmod(piece, pieces // 2)
+            part = slice(half * 2 * P // pieces, (half + 1) * 2 * P // pieces)
             nc.scalar.copy(
-                out=woven[:].rearrange("p (t q i) -> p q t i", t=PACK, i=PACK)[:, part, :, :],
-                in_=raw.rearrange("p i (q t) -> p q t i", t=PACK)[:, part, :, :],
+                out=woven[:].rearrange("p (u e q i) -> p u q i e", u=2, e=2, i=PACK)[:, pair, part, :, :],
+                in_=raw.rearrange("p i (q u e) -> p u q i e", u=2, e=2)[:, pair, part, :, :],
             )
 
         def weave(woven, rows, lo, hi, copy_op=nc.scalar.copy):
@@ -91,9 +92,9 @@ def tile_list_swallow_phase_features_kernel(
         nc.vector.memset(vs[:].bitcast(I32), 0)
         nc.sync.dma_start(out=w2w_raw[:].bitcast(I32), in_=w2_words[0].bitcast(I32))
         nc.sync.dma_start(idx[:], offs)
+        w1_raw0 = load_rows(w1[:, 0:GROUP], "w1_raw0", "X")
         load_scale_rows((nc.sync,) * 4, w2s_raw, w2_scales[0])
         nc.sync.dma_start(out=tabs[0:P:8, :].bitcast(I32), in_=tab_scales[0].bitcast(I32))
-        w1_raw0 = load_rows(w1[:, 0:GROUP], "w1_raw0", "w1_oral_reader")
         nc.sync.dma_start(out=tabw[:], in_=tab_words[0].rearrange("p t i -> p (t i)").bitcast(I32))
 
         def deal_w2_words(a):
@@ -109,7 +110,7 @@ def tile_list_swallow_phase_features_kernel(
             nc.vector.tensor_copy(out=scales[:], in_=raw.rearrange("p (q t) -> p t q", t=PACK))
             return scales
 
-        spread = keep.tile([P, S], U8, name="spread", tag="tabs_w1_oral", align_bytes=64)
+        spread = keep.tile([P, S], U8, name="spread", tag="Y", align_bytes=64)
         nc.vector.tensor_copy(out=spread[:], in_=tabs[:].indirect(idx[:]))
         for r in range(4):
             nc.sync.dma_start(out=vs[r:P:32, :].bitcast(I32), in_=spread[8 * r : P : 32, :].bitcast(I32))
@@ -117,10 +118,10 @@ def tile_list_swallow_phase_features_kernel(
         nc.sync.dma_start(out=gain_sb[:], in_=gain.rearrange("(a p t) -> p a t", a=2, t=PACK))
         w2w = [deal_w2_words(0), deal_w2_words(1)]
         w2s = [deal_bytes(w2s_raw[:, a * GROUP : (a + 1) * GROUP], "w2s%d" % a) for a in range(2)]
-        w1q = [quantise_weight(w1_raw0[:], "w1q0", 1)]
-        oral_sb = [load_rows(oral[0:GROUP, :], "oral0", "w1_oral_reader")]
+        w1q = [quantise_weight(w1_raw0[:], "w1q0", 2)]
+        w1_raw1 = load_rows(w1[:, GROUP : 2 * GROUP], "w1_raw1", "X")
+        oral_sb = [load_rows(oral[0:GROUP, :], "oral0", "Y")]
         nc.sync.dma_start(p1[:], pos1)
-        w1_raw1 = load_rows(w1[:, GROUP : 2 * GROUP], "w1_raw1", "tabs_w1_oral")
         vw = []
         for half in range(2):
             words = keep.tile([P, BANK], U32, name="vw%d" % half, align_bytes=64)
@@ -132,15 +133,6 @@ def tile_list_swallow_phase_features_kernel(
         for a in range(2):
             nc.sync.dma_start(
                 out=wb_raw[:, a, :, :], in_=wb[a * GROUP : (a + 1) * GROUP, :].rearrange("(p i) n -> p i n", i=PACK)
-            )
-        waw_raw = keep.tile([P, 2, N], I32, name="waw_raw", tag="w2w_waw", align_bytes=64)
-        nc.sync.dma_start(out=waw_raw[:], in_=wa_words.rearrange("a p n i -> p a (n i)").bitcast(I32))
-        was_raw = keep.tile([P, N], U8, name="was_raw", tag="w2s_was_bias", align_bytes=64)
-        nc.gpsimd.memset(was_raw[:].bitcast(I32), 0)
-        for quad in range(4):
-            nc.sync.dma_start(
-                out=was_raw[32 * quad : 32 * quad + 8, :].bitcast(I32),
-                in_=wa_scales[:, 4 * quad : 4 * quad + 4, :].bitcast(I32),
             )
 
         def first_stage(a, t):
@@ -163,25 +155,22 @@ def tile_list_swallow_phase_features_kernel(
                 )
                 nc.scalar.copy(out=top[:, cols], in_=sum2[:])
                 nc.vector.tensor_tensor(out=top[:, cols], in0=sum1[:], in1=top[:, cols], op=ALU.max)
-            gained = oral_sb[a][:, t, :]
-            nc.scalar.activation(out=gained, in_=gained, func=ACT.Copy, scale=gain_sb[:, a, t : t + 1])
             return top
 
-        def pick(a, t, top, lo, hi, xa):
-            width = hi - lo
-            cols = slice(lo // LIST, hi // LIST)
-            picked = ring.tile([P, width], F32, name="picked", tag="picked", bufs=3)
-            nc.vector.tensor_copy(out=picked[:], in_=top[:].indirect(p2[:, cols]))
-            bent = ring.tile([P, width], F32, name="bent", tag="bent", bufs=4)
-            nc.scalar.activation(out=bent[:], in_=picked[:], func=ACT.Tanh)
-            nc.vector.tensor_tensor(
-                out=xa[:, t, :], in0=top[:].indirect(p1[:, cols]), in1=oral_sb[a][:, t, lo:hi], op=ALU.mult
-            )
-            return picked[:], bent
+        def pick_pharyngeal(top, lo, hi, picked):
+            nc.vector.tensor_copy(out=picked, in_=top[:].indirect(p2[:, lo // LIST : hi // LIST]))
 
-        def bend(a, t, pair, xb):
+        def pick_oral(a, t, top, lo, hi, xa):
+            nc.vector.tensor_tensor(
+                out=xa[:, t, :], in0=top[:].indirect(p1[:, lo // LIST : hi // LIST]),
+                in1=oral_sb[a][:, t, lo:hi], op=ALU.mult,
+            )
+
+        def bend(a, t, picked, xb):
+            bent = ring.tile([P, picked.shape[1]], F32, name="bent", tag="bent", bufs=4)
+            nc.scalar.activation(out=bent[:], in_=picked, func=ACT.Tanh)
             nc.vector.scalar_tensor_tensor(
-                out=xb[:, t, :], in0=pair[0], scalar=gain_sb[:, a, t : t + 1], in1=pair[1][:],
+                out=xb[:, t, :], in0=picked, scalar=gain_sb[:, a, t : t + 1], in1=bent[:],
                 op0=ALU.mult, op1=ALU.mult,
             )
 
@@ -237,38 +226,59 @@ def tile_list_swallow_phase_features_kernel(
 
         plan("w1q1", weight_piece(w1_raw1[:]))
         plan("wbq0", weight_piece(wb_raw[:, 0, :, :]))
-        counts = COUNTS
-        tops = [first_stage(0, 0)]
+        plan("wbq1", weight_piece(wb_raw[:, 1, :, :]))
+        tops = []
         waq = []
-        pair = None
+        picked = None
         for s in range(2 * PACK):
             a, t = divmod(s, PACK)
-            if s + 1 < 2 * PACK:
-                tops.append(first_stage(*divmod(s + 1, PACK)))
+            width = (J, CHUNKS[0][1])[a]
+            tops.append(first_stage(a, t))
             if s > 0:
-                bend((s - 1) // PACK, (s - 1) % PACK, pair, (xs0, xs1)[(s - 1) // PACK][1])
-            pair = pick(a, t, tops[s], 0, (J, CHUNKS[0][1])[a], (xs0, xs1)[a][0])
+                bend((s - 1) // PACK, (s - 1) % PACK, picked, (xs0, xs1)[(s - 1) // PACK][1])
+            gained = oral_sb[a][:, t, :]
+            nc.scalar.activation(out=gained, in_=gained, func=ACT.Copy, scale=gain_sb[:, a, t : t + 1])
+            picked_tile = ring.tile([P, width], F32, name="picked", tag="picked", bufs=3)
+            picked = picked_tile[:]
+            pick_pharyngeal(tops[s], 0, width, picked)
+            pick_oral(a, t, tops[s], 0, width, (xs0, xs1)[a][0])
             if s == PACK:
-                plan("xa0", rows_piece(xs0[0]))
                 plan("xb0", rows_piece(xs0[1]))
-                plan("wbq1", weight_piece(wb_raw[:, 1, :, :]))
-            run_long_copies(counts[s])
-            if s == 2:
+                plan("xa0", rows_piece(xs0[0]))
+            run_long_copies(COUNTS[s])
+            if s == 1:
                 w1q.append(made["w1q1"])
-                oral_sb.append(load_rows(oral[GROUP : 2 * GROUP, :], "oral1", "tabs_w1_oral"))
+                oral_sb.append(load_rows(oral[GROUP : 2 * GROUP, :], "oral1", "X"))
             if s == PACK - 1:
-                reader_sb = load_rows(reader, "reader_sb", "w1_oral_reader")
+                waw_raw = keep.tile([P, 2, N], I32, name="waw_raw", tag="Y", align_bytes=64)
+                nc.sync.dma_start(out=waw_raw[:], in_=wa_words.rearrange("a p n i -> p a (n i)").bitcast(I32))
             if s == PACK:
-                was = deal_bytes(was_raw[:], "was")
-                bias_sb = keep.tile([P, PACK], F32, name="bias_sb", tag="w2s_was_bias", align_bytes=64)
-                nc.sync.dma_start(out=bias_sb[:], in_=bias.rearrange("(p t) -> p t", t=PACK))
+                was_raw = keep.tile([P, N], U8, name="was_raw", tag="tabw_wb", align_bytes=64)
+                nc.gpsimd.memset(was_raw[:].bitcast(I32), 0)
+                for quad in range(4):
+                    nc.sync.dma_start(
+                        out=was_raw[32 * quad : 32 * quad + 8, :].bitcast(I32),
+                        in_=wa_scales[:, 4 * quad : 4 * quad + 4, :].bitcast(I32),
+                    )
+            if s == PACK + 1:
+                waw = []
                 for g in range(2):
                     words = keep.tile([P, PACK, P], I32, name="waw%d" % g, align_bytes=64)
-                    nc.vector.tensor_copy(out=words[:], in_=waw_raw[:, g, :].rearrange("p (q t) -> p t q", t=PACK))
+                    nc.vector.tensor_copy(
+                        out=words[:].rearrange("p (u e) q -> p u q e", e=2),
+                        in_=waw_raw[:, g, :].rearrange("p (q u e) -> p u q e", u=2, e=2),
+                    )
+                    waw.append(words)
+                reader_sb = load_rows(reader, "reader_sb", "Y")
+            if s == PACK + 2:
+                was = deal_bytes(was_raw[:], "was")
+                bias_sb = keep.tile([P, PACK], F32, name="bias_sb", tag="tabw_wb", align_bytes=64)
+                nc.sync.dma_start(out=bias_sb[:], in_=bias.rearrange("(p t) -> p t", t=PACK))
+                for g in range(2):
                     waq.append((
-                        words[:].rearrange("p t q -> p (t q)"), was[4 * g : P, :, :].rearrange("p t q -> p (t q)")
+                        waw[g][:].rearrange("p t q -> p (t q)"), was[4 * g : P, :, :].rearrange("p t q -> p (t q)")
                     ))
-        bend(1, PACK - 1, pair, xs1[1])
+        bend(1, PACK - 1, picked, xs1[1])
         wbq = [made["wbq0"], made["wbq1"]]
         x0q = [made["xa0"], made["xb0"]]
         tops = tops[PACK:]
@@ -305,7 +315,8 @@ def tile_list_swallow_phase_features_kernel(
                     out=y[:, t, :], in0=banks[c][t // per_bank][:, t % per_bank, :], scalar=bias_sb[:, t : t + 1],
                     in1=reader_sb[:, t, lo:hi], op0=ALU.add, op1=ALU.mult,
                 )
-            nc.sync.dma_start(out=out_rows[:, :, lo:hi], in_=y[:])
+                if t % 2 == 1:
+                    nc.sync.dma_start(out=out_rows[:, t - 1 : t + 1, lo:hi], in_=y[:, t - 1 : t + 1, :])
             woven = woven_tile(hi - lo)
             if shared:
                 shared_weave(woven, y, hi - lo)
@@ -315,25 +326,18 @@ def tile_list_swallow_phase_features_kernel(
             nc.sync.dma_start(out=out_words[:, lo:hi], in_=y_codes[:, lo:hi].bitcast(I32))
 
         lo, hi = CHUNKS[1]
-        late = keep.tile([P, 2, PACK, hi - lo], F32, name="late", tag="tabw_wb", align_bytes=64)
+        late = ring.tile([P, 2, PACK, hi - lo], F32, name="late", tag="xa")
         xb = ring.tile([P, PACK, hi - lo], BF16, name="xb", tag="xb")
-        cols = slice(lo // LIST, hi // LIST)
-        pairs = []
         for t in range(PACK):
-            nc.vector.tensor_copy(out=late[:, 1, t, :], in_=tops[t][:].indirect(p2[:, cols]))
-            bent = ring.tile([P, hi - lo], F32, name="bent", tag="bent", bufs=4)
-            nc.scalar.activation(out=bent[:], in_=late[:, 1, t, :], func=ACT.Tanh)
-            pairs.append((late[:, 1, t, :], bent))
+            pick_pharyngeal(tops[t], lo, hi, late[:, 1, t, :])
             if t == 1:
                 product(0, xa1, waq[1], False, False)
             if t == 3:
                 product(0, xb1, wbq[1], True, False)
         for t in range(PACK):
-            bend(1, t, pairs[t], xb)
+            bend(1, t, late[:, 1, t, :], xb)
         for t in range(PACK):
-            nc.vector.tensor_tensor(
-                out=late[:, 0, t, :], in0=tops[t][:].indirect(p1[:, cols]), in1=oral_sb[1][:, t, lo:hi], op=ALU.mult
-            )
+            pick_oral(1, t, tops[t], lo, hi, late[:, 0, :, :])
             if t == 0:
                 product(1, xb, wbq[1], False, False)
             if t == 1:

from contextlib import ExitStack

import concourse.mybir as mybir

K, H, N, T, S, J = 512, 1024, 512, 4096, 1024, 512
FLOPS = 2 * (2 * K * H * S + 2 * H * N * J)

F32 = mybir.dt.float32
BF16 = mybir.dt.bfloat16
I32 = mybir.dt.int32
U32 = mybir.dt.uint32
U16 = mybir.dt.uint16
U8 = mybir.dt.uint8
FP8X4 = mybir.dt.float8_e4m3fn_x4
FP4X4 = mybir.dt.float4_e2m1fn_x4
ALU = mybir.AluOpType
ACT = mybir.ActivationFunctionType

P = 128
PACK = 4
GROUP = P * PACK
BANK = 512
LIST = 16
CHUNKS = ((0, 256), (256, 512))
PIECES = 4
SCALAR_SHARE = 3
COUNTS = (2, 3, 3, 3, 3, 2, 2, 2)


def load_scale_rows(queues, plane, rows):
    for r, queue in enumerate(queues):
        queue.dma_start(out=plane[r:P:32, :].bitcast(I32), in_=rows[r:16:4, :].bitcast(I32))


def tile_list_swallow_phase_features_kernel(
    tc, tab_words, tab_scales, offs, pos1, pos2, w1, w2_words, w2_scales, gain, oral,
    wa_words, wa_scales, wb, bias, reader, out_0, out_1, out_2,
):
    nc = tc.nc
    with ExitStack() as ctx:
        keep = ctx.enter_context(tc.tile_pool(name="keep", bufs=1))
        ring = ctx.enter_context(tc.tile_pool(name="ring", bufs=2))
        psum = ctx.enter_context(tc.psum_pool(name="psum", bufs=1))

        idx = keep.tile([P, S // LIST], U16, name="idx")
        p1 = keep.tile([P, J // LIST], U16, name="p1")
        p2 = keep.tile([P, J // LIST], U16, name="p2")

        tabw = keep.tile([P, T], I32, name="tabw", tag="tabw_wb", align_bytes=64)
        tabs = keep.tile([P, T], U8, name="tabs", align_bytes=64)
        w2w_raw = keep.tile([P, 2 * H], U8, name="w2w_raw", align_bytes=64)
        w2s_raw = keep.tile([P, H], U8, name="w2s_raw", align_bytes=64)
        gain_sb = keep.tile([P, 2, PACK], F32, name="gain_sb")

        def load_rows(rows, name, tag):
            dealt = keep.tile([P, PACK, GROUP], F32, name=name, tag=tag, align_bytes=64)
            nc.sync.dma_start(out=dealt[:], in_=rows.rearrange("(p t) j -> p t j", t=PACK))
            return dealt

        def quantise(woven, width, name):
            codes = keep.tile([P, width], U32, name=name + "_codes", align_bytes=64)
            scales = keep.tile([P, width], U8, name=name + "_scales", align_bytes=64)
            nc.vector.quantize_mx(out=codes[:].bitcast(FP8X4), scales=scales[:], in_=woven[:])
            return codes, scales

        def woven_tile(width):
            return ring.tile([P, width * PACK], BF16, name="woven", tag="woven", bufs=5, align_bytes=64)

        def deal_weight(woven, raw, piece, pieces):
            pair, half = divmod(piece, pieces // 2)
            part = slice(half * 2 * P // pieces, (half + 1) * 2 * P // pieces)
            nc.scalar.copy(
                out=woven[:].rearrange("p (u e q i) -> p u q i e", u=2, e=2, i=PACK)[:, pair, part, :, :],
                in_=raw.rearrange("p i (q u e) -> p u q i e", u=2, e=2)[:, pair, part, :, :],
            )

        def weave(woven, rows, lo, hi, copy_op=nc.scalar.copy):
            copy_op(
                out=woven[:, lo * PACK : hi * PACK].rearrange("p (c i t) -> p c t i", i=PACK, t=PACK),
                in_=rows[:, :, lo:hi].rearrange("p t (c i) -> p c t i", i=PACK),
            )

        def quantise_weight(raw, name, pieces):
            woven = woven_tile(GROUP)
            for piece in range(pieces):
                deal_weight(woven, raw, piece, pieces)
            return quantise(woven, GROUP, name)

        nc.gpsimd.memset(tabs[:].bitcast(I32), 0)
        nc.vector.memset(w2s_raw[:].bitcast(I32), 0)
        vs = keep.tile([P, S], U8, name="vs", align_bytes=64)
        nc.vector.memset(vs[:].bitcast(I32), 0)
        nc.sync.dma_start(out=w2w_raw[:].bitcast(I32), in_=w2_words[0].bitcast(I32))
        nc.sync.dma_start(idx[:], offs)
        w1_raw0 = load_rows(w1[:, 0:GROUP], "w1_raw0", "X")
        load_scale_rows((nc.sync,) * 4, w2s_raw, w2_scales[0])
        nc.sync.dma_start(out=tabs[0:P:8, :].bitcast(I32), in_=tab_scales[0].bitcast(I32))
        nc.sync.dma_start(out=tabw[:], in_=tab_words[0].rearrange("p t i -> p (t i)").bitcast(I32))

        def deal_w2_words(a):
            words = keep.tile([P, PACK, P, 2], U8, name="w2w%d" % a, align_bytes=64)
            nc.vector.tensor_copy(
                out=words[:],
                in_=w2w_raw[:, 2 * a * GROUP : 2 * (a + 1) * GROUP].rearrange("p (q t b) -> p t q b", t=PACK, b=2),
            )
            return words

        def deal_bytes(raw, name):
            scales = keep.tile([P, PACK, P], U8, name=name, align_bytes=64)
            nc.vector.tensor_copy(out=scales[:], in_=raw.rearrange("p (q t) -> p t q", t=PACK))
            return scales

        spread = keep.tile([P, S], U8, name="spread", tag="Y", align_bytes=64)
        nc.vector.tensor_copy(out=spread[:], in_=tabs[:].indirect(idx[:]))
        for r in range(4):
            nc.sync.dma_start(out=vs[r:P:32, :].bitcast(I32), in_=spread[8 * r : P : 32, :].bitcast(I32))
        nc.sync.dma_start(p2[:], pos2)
        nc.sync.dma_start(out=gain_sb[:], in_=gain.rearrange("(a p t) -> p a t", a=2, t=PACK))
        w2w = [deal_w2_words(0), deal_w2_words(1)]
        w2s = [deal_bytes(w2s_raw[:, a * GROUP : (a + 1) * GROUP], "w2s%d" % a) for a in range(2)]
        w1q = [quantise_weight(w1_raw0[:], "w1q0", 2)]
        w1_raw1 = load_rows(w1[:, GROUP : 2 * GROUP], "w1_raw1", "X")
        oral_sb = [load_rows(oral[0:GROUP, :], "oral0", "Y")]
        nc.sync.dma_start(p1[:], pos1)
        vw = []
        for half in range(2):
            words = keep.tile([P, BANK], U32, name="vw%d" % half, align_bytes=64)
            cols = slice(half * BANK // LIST, (half + 1) * BANK // LIST)
            nc.vector.tensor_copy(out=words[:], in_=tabw[:].bitcast(U32).indirect(idx[:, cols]))
            vw.append(words)

        wb_raw = keep.tile([P, 2, PACK, N], F32, name="wb_raw", tag="tabw_wb", align_bytes=64)
        for a in range(2):
            nc.sync.dma_start(
                out=wb_raw[:, a, :, :], in_=wb[a * GROUP : (a + 1) * GROUP, :].rearrange("(p i) n -> p i n", i=PACK)
            )

        def first_stage(a, t):
            top = ring.tile([P, S], F32, name="top%d%d" % (a, t), tag="top", bufs=6)
            for half in range(2):
                cols = slice(half * BANK, (half + 1) * BANK)
                sum1 = psum.tile([P, BANK], F32, name="sum1", tag="sum1", bufs=2)
                sum2 = psum.tile([P, BANK], F32, name="sum2", tag="sum2", bufs=2)
                nc.tensor.matmul_mx(
                    out=sum2[:],
                    lhsT=w2w[a][:, t, :, :].rearrange("p q b -> p (q b)").bitcast(FP4X4),
                    lhsT_scale=w2s[a][:, t, :],
                    rhs=vw[half][:].bitcast(FP8X4), rhs_scale=vs[:, cols], start=True, stop=True,
                )
                nc.tensor.matmul_mx(
                    out=sum1[:],
                    lhsT=w1q[a][0][:, t * P : (t + 1) * P].bitcast(FP8X4),
                    lhsT_scale=w1q[a][1][:, t * P : (t + 1) * P],
                    rhs=vw[half][:].bitcast(FP8X4), rhs_scale=vs[:, cols], start=True, stop=True,
                )
                nc.scalar.copy(out=top[:, cols], in_=sum2[:])
                nc.vector.tensor_tensor(out=top[:, cols], in0=sum1[:], in1=top[:, cols], op=ALU.max)
            return top

        def pick_pharyngeal(top, lo, hi, picked):
            nc.vector.tensor_copy(out=picked, in_=top[:].indirect(p2[:, lo // LIST : hi // LIST]))

        def pick_oral(a, t, top, lo, hi, xa):
            nc.vector.tensor_tensor(
                out=xa[:, t, :], in0=top[:].indirect(p1[:, lo // LIST : hi // LIST]),
                in1=oral_sb[a][:, t, lo:hi], op=ALU.mult,
            )

        def bend(a, t, picked, xb):
            bent = ring.tile([P, picked.shape[1]], F32, name="bent", tag="bent", bufs=4)
            nc.scalar.activation(out=bent[:], in_=picked, func=ACT.Tanh)
            nc.vector.scalar_tensor_tensor(
                out=xb[:, t, :], in0=picked, scalar=gain_sb[:, a, t : t + 1], in1=bent[:],
                op0=ALU.mult, op1=ALU.mult,
            )

        def x_tiles(width):
            xa = ring.tile([P, PACK, width], F32, name="xa", tag="xa")
            xb = ring.tile([P, PACK, width], BF16, name="xb", tag="xb")
            return xa, xb

        banks = []
        for c, (lo, hi) in enumerate(CHUNKS):
            per_bank = BANK // (hi - lo)
            banks.append([
                psum.tile([P, per_bank, hi - lo], F32, name="e%d%d" % (c, b)) for b in range(PACK // per_bank)
            ])

        def second_pass(c, weight, x, x_lo, first, last):
            lo, hi = CHUNKS[c]
            per_bank = BANK // (hi - lo)
            cols = slice(lo - x_lo, hi - x_lo)
            for t in range(PACK):
                nc.tensor.matmul_mx(
                    out=banks[c][t // per_bank][:, t % per_bank, :],
                    lhsT=weight[0][:, t * P : (t + 1) * P].bitcast(FP8X4),
                    lhsT_scale=weight[1][:, t * P : (t + 1) * P],
                    rhs=x[0][:, cols].bitcast(FP8X4), rhs_scale=x[1][:, cols],
                    start=first and t % per_bank == 0, stop=last and t % per_bank == per_bank - 1,
                )

        xs0 = x_tiles(J)
        xs1 = x_tiles(CHUNKS[0][1])
        long_copies = []
        made = {}

        def plan(name, copy_piece):
            woven = woven_tile(GROUP)
            for piece in range(PIECES):
                long_copies.append((name, woven, copy_piece, piece))

        def run_long_copies(count):
            for name, woven, copy_piece, piece in long_copies[:count]:
                copy_piece(woven, piece)
                if piece == PIECES - 1:
                    made[name] = quantise(woven, GROUP, name)
            del_count = long_copies[count:]
            long_copies.clear()
            long_copies.extend(del_count)

        def weight_piece(raw):
            return lambda woven, piece: deal_weight(woven, raw, piece, PIECES)

        def rows_piece(rows):
            return lambda woven, piece: weave(woven, rows, piece * J // PIECES, (piece + 1) * J // PIECES)

        plan("w1q1", weight_piece(w1_raw1[:]))
        plan("wbq0", weight_piece(wb_raw[:, 0, :, :]))
        plan("wbq1", weight_piece(wb_raw[:, 1, :, :]))
        tops = []
        waq = []
        picked = None
        for s in range(2 * PACK):
            a, t = divmod(s, PACK)
            width = (J, CHUNKS[0][1])[a]
            tops.append(first_stage(a, t))
            if s > 0:
                bend((s - 1) // PACK, (s - 1) % PACK, picked, (xs0, xs1)[(s - 1) // PACK][1])
            gained = oral_sb[a][:, t, :]
            nc.scalar.activation(out=gained, in_=gained, func=ACT.Copy, scale=gain_sb[:, a, t : t + 1])
            picked_tile = ring.tile([P, width], F32, name="picked", tag="picked", bufs=3)
            picked = picked_tile[:]
            pick_pharyngeal(tops[s], 0, width, picked)
            pick_oral(a, t, tops[s], 0, width, (xs0, xs1)[a][0])
            if s == PACK:
                plan("xb0", rows_piece(xs0[1]))
                plan("xa0", rows_piece(xs0[0]))
            run_long_copies(COUNTS[s])
            if s == 1:
                w1q.append(made["w1q1"])
                oral_sb.append(load_rows(oral[GROUP : 2 * GROUP, :], "oral1", "X"))
            if s == PACK - 1:
                waw_raw = keep.tile([P, 2, N], I32, name="waw_raw", tag="Y", align_bytes=64)
                nc.sync.dma_start(out=waw_raw[:], in_=wa_words.rearrange("a p n i -> p a (n i)").bitcast(I32))
            if s == PACK:
                was_raw = keep.tile([P, N], U8, name="was_raw", tag="tabw_wb", align_bytes=64)
                nc.gpsimd.memset(was_raw[:].bitcast(I32), 0)
                for quad in range(4):
                    nc.sync.dma_start(
                        out=was_raw[32 * quad : 32 * quad + 8, :].bitcast(I32),
                        in_=wa_scales[:, 4 * quad : 4 * quad + 4, :].bitcast(I32),
                    )
            if s == PACK + 1:
                waw = []
                for g in range(2):
                    words = keep.tile([P, PACK, P], I32, name="waw%d" % g, align_bytes=64)
                    nc.vector.tensor_copy(
                        out=words[:].rearrange("p (u e) q -> p u q e", e=2),
                        in_=waw_raw[:, g, :].rearrange("p (q u e) -> p u q e", u=2, e=2),
                    )
                    waw.append(words)
                reader_sb = load_rows(reader, "reader_sb", "Y")
            if s == PACK + 2:
                was = deal_bytes(was_raw[:], "was")
                bias_sb = keep.tile([P, PACK], F32, name="bias_sb", tag="tabw_wb", align_bytes=64)
                nc.sync.dma_start(out=bias_sb[:], in_=bias.rearrange("(p t) -> p t", t=PACK))
                for g in range(2):
                    waq.append((
                        waw[g][:].rearrange("p t q -> p (t q)"), was[4 * g : P, :, :].rearrange("p t q -> p (t q)")
                    ))
        bend(1, PACK - 1, picked, xs1[1])
        wbq = [made["wbq0"], made["wbq1"]]
        x0q = [made["xa0"], made["xb0"]]
        tops = tops[PACK:]
        xa1, xb1 = xs1
        for c in range(len(CHUNKS)):
            second_pass(c, waq[0], x0q[0], 0, True, False)
            second_pass(c, wbq[0], x0q[1], 0, False, False)

        out_rows = out_0.rearrange("(p t) j -> p t j", t=PACK)
        out_words = out_1[0].rearrange("p m t -> p (m t)").bitcast(I32)
        y_codes = keep.tile([P, J], U32, name="y_codes", align_bytes=64)
        y_scales = keep.tile([P, J], U8, name="y_scales", align_bytes=64)

        def shared_weave(woven, rows, width):
            cut = width * SCALAR_SHARE // 8
            weave(woven, rows, 0, cut)
            weave(woven, rows, cut, width, nc.vector.tensor_copy)

        def product(c, x, weight, last, shared):
            lo, hi = CHUNKS[c]
            woven = woven_tile(hi - lo)
            if shared:
                shared_weave(woven, x, hi - lo)
            else:
                weave(woven, x, 0, hi - lo)
            second_pass(c, weight, quantise(woven, hi - lo, "x1q%d%d" % (c, last)), lo, False, last)

        def finish_output(c, shared):
            lo, hi = CHUNKS[c]
            per_bank = BANK // (hi - lo)
            y = keep.tile([P, PACK, hi - lo], F32, name="y%d" % c)
            for t in range(PACK):
                nc.vector.scalar_tensor_tensor(
                    out=y[:, t, :], in0=banks[c][t // per_bank][:, t % per_bank, :], scalar=bias_sb[:, t : t + 1],
                    in1=reader_sb[:, t, lo:hi], op0=ALU.add, op1=ALU.mult,
                )
                if t % 2 == 1:
                    nc.sync.dma_start(out=out_rows[:, t - 1 : t + 1, lo:hi], in_=y[:, t - 1 : t + 1, :])
            woven = woven_tile(hi - lo)
            if shared:
                shared_weave(woven, y, hi - lo)
            else:
                weave(woven, y, 0, hi - lo)
            nc.vector.quantize_mx(out=y_codes[:, lo:hi].bitcast(FP8X4), scales=y_scales[:, lo:hi], in_=woven[:])
            nc.sync.dma_start(out=out_words[:, lo:hi], in_=y_codes[:, lo:hi].bitcast(I32))

        lo, hi = CHUNKS[1]
        late = ring.tile([P, 2, PACK, hi - lo], F32, name="late", tag="xa")
        xb = ring.tile([P, PACK, hi - lo], BF16, name="xb", tag="xb")
        for t in range(PACK):
            pick_pharyngeal(tops[t], lo, hi, late[:, 1, t, :])
            if t == 1:
                product(0, xa1, waq[1], False, False)
            if t == 3:
                product(0, xb1, wbq[1], True, False)
        for t in range(PACK):
            bend(1, t, late[:, 1, t, :], xb)
        for t in range(PACK):
            pick_oral(1, t, tops[t], lo, hi, late[:, 0, :, :])
            if t == 0:
                product(1, xb, wbq[1], False, False)
            if t == 1:
                finish_output(0, False)
        product(1, late[:, 0, :, :], waq[1], True, True)
        finish_output(1, True)
        for r in range(4):
            queue = nc.scalar if r % 2 else nc.sync
            queue.dma_start(out=out_2[0, r:16:4, :].bitcast(I32), in_=y_scales[r:P:32, :].bitcast(I32))
